import numpy as np
import ml_dtypes


def mxq(x, axis, fmt="e4m3"):
    dtype, down = {"e4m3": (ml_dtypes.float8_e4m3fn, 7), "e5m2": (ml_dtypes.float8_e5m2, 14)}[fmt]
    v = np.moveaxis(np.asarray(x, np.float32).astype(ml_dtypes.bfloat16).astype(np.float64), axis, -1)
    blocks = v.reshape(v.shape[:-1] + (-1, 32))
    amax = np.abs(blocks).max(-1, keepdims=True)
    byte = np.maximum(np.where(amax > 0, np.frexp(amax)[1] - 1 + 127, 0) - down, 1)
    scale = np.exp2(byte - 127.0)
    codes = (blocks / scale).astype(np.float32).astype(dtype).astype(np.float64)
    return np.moveaxis((codes * scale).reshape(v.shape), -1, axis)


WIDE = False


def mx_kscale(k):
    if not WIDE:
        return np.ones(k)
    levels = np.array([30, -30])
    if k % 512:
        return np.exp2(np.random.permutation(np.resize(levels, k // 32))).repeat(32)
    a = np.empty((k // 512, 16))
    for p in range(k // 512):
        a[p, :8] = np.random.permutation(np.resize(levels, 8))
        for g in range(8):
            far = levels[np.abs(levels - a[p, g]) >= 10]
            a[p, g + 8] = far[np.random.randint(len(far))]
    return np.exp2(a.ravel()).repeat(32)


def f64(x):
    return np.asarray(x).astype(np.float64)


def striped(idx):
    return np.tile(idx.reshape(-1, 16).T, (8, 1)).astype(np.uint16)


def unstriped(offs):
    return offs[:16].T.reshape(-1).astype(np.int64)


E2M1 = np.array([0.0, 0.5, 1.0, 1.5, 2.0, 3.0, 4.0, 6.0, -0.0, -0.5, -1.0, -1.5, -2.0, -3.0, -4.0, -6.0])


def pack_weight(w, fmt):
    k, n = w.shape
    w = f64(np.asarray(w, np.float32).astype(ml_dtypes.bfloat16)).reshape(k // 32, 32, n)
    amax = np.abs(w).max(1)
    if fmt == "e4m3":
        byte = np.frexp(amax)[1] - 1 + 127 - 7
    else:
        mant, ex = np.frexp(amax / 6.0)
        byte = np.where(mant > 0.5, ex, ex - 1) + 127
    byte = np.clip(np.where(amax > 0, byte, 1), 1, 254)
    scaled = (w * np.exp2(127.0 - byte)[:, None, :]).reshape(k, n).astype(np.float32)
    by_word = np.ascontiguousarray(scaled.reshape(k // 512, 128, 4, n).transpose(0, 1, 3, 2))
    if fmt == "e4m3":
        words = by_word.astype(ml_dtypes.float8_e4m3fn).view(np.uint8)
    else:
        c = by_word.astype(ml_dtypes.float4_e2m1fn).view(np.uint8) & 0xF
        words = (c[..., 0::2] | (c[..., 1::2] << 4)).reshape(k // 512, 128, 2 * n)
    return np.ascontiguousarray(words), np.ascontiguousarray(byte.astype(np.uint8).reshape(k // 512, 16, n))


def unpack_weight(words, scales, fmt):
    g, _, n = scales.shape
    words = np.ascontiguousarray(words).reshape(g, 128, n, -1)
    if fmt == "e4m3":
        vals = words.view(ml_dtypes.float8_e4m3fn).astype(np.float64)
    else:
        nib = np.empty((g, 128, n, 4), np.uint8)
        nib[..., 0::2] = words & 0xF
        nib[..., 1::2] = words >> 4
        vals = E2M1[nib]
    vals = vals * np.repeat(np.exp2(scales.astype(np.float64) - 127.0), 8, axis=1)[..., None]
    return vals.transpose(0, 1, 3, 2).reshape(g * 512, n)


def relu(v):
    return np.maximum(v, 0.0)


def d_relu(v):
    return (v > 0).astype(np.float64)


K, T, E, C, H, N = 256, 2048, 4, 512, 512, 512


def by_expert(wq, xq):
    return np.concatenate([wq[e].T @ xq[:, e * C:(e + 1) * C] for e in range(E)], axis=1)


def setup_inputs():
    n = np.random.standard_normal
    s = mx_kscale(N)[:, None]
    u = mx_kscale(H)
    w2 = [pack_weight(m, "e2m1") for m in n((E, N, H)) / np.sqrt(N) / s[None] * u[None, None, :]]
    w1 = [pack_weight(m, "e2m1") for m in n((E, H, K)) / np.sqrt(H) / u[None, :, None]]
    w3 = [pack_weight(m, "e2m1") for m in n((E, H, K)) / np.sqrt(H) / u[None, :, None]]
    return {
        "dyT": (n((N, T)) * s).astype(np.float32),
        "a1": n((H, E * C)).astype(np.float32),
        "a3": n((H, E * C)).astype(np.float32),
        "w2_words": np.stack([m[0] for m in w2]),
        "w2_scales": np.stack([m[1] for m in w2]),
        "w1_words": np.stack([m[0] for m in w1]),
        "w1_scales": np.stack([m[1] for m in w1]),
        "w3_words": np.stack([m[0] for m in w3]),
        "w3_scales": np.stack([m[1] for m in w3]),
        "gate": np.tile(np.random.uniform(0.2, 1.0, E * C), (N, 1)).astype(np.float32),
        "offs": striped(np.random.permutation(T)[:E * C]),
    }


def reference(dyT, a1, a3, w2_words, w2_scales, w1_words, w1_scales, w3_words, w3_scales, gate, offs):
    idx = unstriped(offs)
    w2 = np.stack([unpack_weight(w2_words[e], w2_scales[e], "e2m1") for e in range(E)])
    w1 = np.stack([unpack_weight(w1_words[e], w1_scales[e], "e2m1") for e in range(E)])
    w3 = np.stack([unpack_weight(w3_words[e], w3_scales[e], "e2m1") for e in range(E)])
    gq = mxq(f64(gate) * f64(dyT)[:, idx], 0, "e5m2")
    dh = by_expert(w2, gq)
    da1 = dh * f64(a3) * d_relu(f64(a1))
    da3 = dh * relu(f64(a1))
    dx = by_expert(w1, mxq(da1, 0, "e5m2")) + by_expert(w3, mxq(da3, 0, "e5m2"))
    out = np.zeros((K, T))
    out[:, idx] = dx
    return out

@@ -1,0 +1,171 @@
+from contextlib import ExitStack
+
+import concourse.mybir as mybir
+
+K, T, E, C, H, N = 256, 2048, 4, 512, 512, 512
+P = 128
+PACK = 4
+
+FLOPS = 2 * E * C * (N * H + 2 * H * K)
+BYTES = 4 * (N * T + 2 * H * E * C + E * C + K * T) + E * (N * H + 2 * H * K) // 2 + E * (N * H + 2 * H * K) // 32 + 2 * P * T // 16
+
+F32 = mybir.dt.float32
+BF16 = mybir.dt.bfloat16
+I32 = mybir.dt.int32
+U32 = mybir.dt.uint32
+U16 = mybir.dt.uint16
+U8 = mybir.dt.uint8
+E5M2X4 = mybir.dt.float8_e5m2_x4
+E2M1X4 = mybir.dt.float4_e2m1fn_x4
+ALU = mybir.AluOpType
+COPY = mybir.ActivationFunctionType.Copy
+
+
+def tile_moe_bdx_glu_relu_kernel(
+    tc, dyT, a1, a3, w2_words, w2_scales, w1_words, w1_scales, w3_words, w3_scales, gate, offs, out
+):
+    nc = tc.nc
+    with ExitStack() as ctx:
+        held = ctx.enter_context(tc.tile_pool(name="held", bufs=1))
+        ring = ctx.enter_context(tc.tile_pool(name="ring", bufs=2))
+        dx_ring = ctx.enter_context(tc.tile_pool(name="dx_ring", bufs=6))
+        dh_banks = ctx.enter_context(tc.psum_pool(name="dh_banks", bufs=6))
+        dx_banks = ctx.enter_context(tc.psum_pool(name="dx_banks", bufs=2))
+
+        offsets = held.tile([P, E * C // 16], U16, name="offsets")
+        nc.sync.dma_start(offsets[:], offs)
+
+        def load_scales(plane, dram):
+            for q in range(4):
+                nc.sync.dma_start(
+                    plane[32 * q : 32 * q + 4].bitcast(I32),
+                    dram[:, 0, 4 * q : 4 * q + 4, :].rearrange("e f i -> f e i").bitcast(I32),
+                )
+
+        w2_raw = held.tile([P, E, 2 * H], U8, name="w2_raw", align_bytes=64)
+        w2_raw_scale = held.tile([P, E, H], U8, name="w2_raw_scale", align_bytes=64)
+        w2_code = held.tile([P, E, 2 * H], U8, name="w2_code", align_bytes=64)
+        w2_scale = held.tile([P, E, H], U8, name="w2_scale", align_bytes=64)
+        w1_code = held.tile([P, E, 2 * K], U8, name="w1_code", align_bytes=64)
+        w3_code = held.tile([P, E, 2 * K], U8, name="w3_code", align_bytes=64)
+        w1_scale = held.tile([P, E, K], U8, name="w1_scale", align_bytes=64)
+        w3_scale = held.tile([P, E, K], U8, name="w3_scale", align_bytes=64)
+        for plane in (w2_raw_scale, w1_scale, w3_scale):
+            nc.vector.memset(plane[:].bitcast(I32), 0)
+
+        gates = held.tile([P, E * C], F32, name="gates")
+        planes = [held.tile([P, T], F32, name=f"dy_{j}") for j in range(PACK)]
+        a1_t = [held.tile([P, PACK, C], F32, name=f"a1_{e}") for e in range(E)]
+        a3_t = [held.tile([P, PACK, C], F32, name=f"a3_{e}") for e in range(E)]
+
+        def slots(e):
+            return slice(e * C, (e + 1) * C)
+
+        def load_saved(e):
+            nc.sync.dma_start(a1_t[e][:], a1.rearrange("(p t) s -> p t s", t=PACK)[:, :, slots(e)])
+            nc.sync.dma_start(a3_t[e][:], a3.rearrange("(p t) s -> p t s", t=PACK)[:, :, slots(e)])
+
+        nc.sync.dma_start(w2_raw[:].bitcast(I32), w2_words.rearrange("e s p b -> p (e s) b").bitcast(I32))
+        load_scales(w2_raw_scale, w2_scales)
+        nc.sync.dma_start(gates[:, 0 : 2 * C], gate[0:P, 0 : 2 * C])
+        for j in range(PACK):
+            nc.sync.dma_start(planes[j][:], dyT.rearrange("(p j) s -> p j s", j=PACK)[:, j, :])
+        load_saved(0)
+        nc.sync.dma_start(gates[:, 2 * C : 4 * C], gate[0:P, 2 * C : 4 * C])
+        nc.sync.dma_start(w1_code[:].bitcast(I32), w1_words.rearrange("e s p b -> p (e s) b").bitcast(I32))
+        nc.sync.dma_start(w3_code[:].bitcast(I32), w3_words.rearrange("e s p b -> p (e s) b").bitcast(I32))
+        load_scales(w1_scale, w1_scales)
+        load_scales(w3_scale, w3_scales)
+        for e in range(1, E):
+            load_saved(e)
+
+        nc.vector.tensor_copy(
+            w2_code[:].bitcast(U16).rearrange("p e (t m) -> p e t m", t=PACK),
+            w2_raw[:].bitcast(U16).rearrange("p e (m t) -> p e t m", t=PACK),
+        )
+        nc.vector.tensor_copy(
+            w2_scale[:].rearrange("p e (t m) -> p e t m", t=PACK),
+            w2_raw_scale[:].rearrange("p e (m t) -> p e t m", t=PACK),
+        )
+
+        def interleave(dst, src):
+            nc.scalar.activation(
+                dst.rearrange("p (c i) t -> p c t i", i=4), src.rearrange("p t (c i) -> p c t i", i=4), COPY
+            )
+
+        def quantise(values, kind):
+            code = ring.tile([P, C], U32, name=f"{kind}_code", align_bytes=64)
+            scale = ring.tile([P, C], U8, name=f"{kind}_scale", align_bytes=64)
+            nc.vector.quantize_mx(
+                out=code[:].bitcast(E5M2X4), scales=scale[:], in_=values.rearrange("p c t -> p (c t)")
+            )
+            return code, scale
+
+        dx = {}
+
+        def chain(e):
+            idx = offsets[:, e * (C // 16) : (e + 1) * (C // 16)]
+            g4 = ring.tile([P, PACK, C], F32, name="g4")
+            for j in range(PACK):
+                nc.vector.tensor_tensor(g4[:, j, :], planes[j][:].indirect(idx), gates[:, slots(e)], ALU.mult)
+            g_mix = ring.tile([P, C, PACK], BF16, name="g_mix", align_bytes=64)
+            interleave(g_mix[:], g4[:])
+            g_code, g_scale = quantise(g_mix[:], "g")
+
+            nc.vector.scalar_tensor_tensor(a3_t[e][:], a1_t[e][:], 0.0, a3_t[e][:], ALU.is_gt, ALU.mult)
+
+            y1 = ring.tile([P, PACK, C], BF16, name="y1")
+            y3 = ring.tile([P, PACK, C], BF16, name="y3")
+            for t in range(PACK):
+                dh = dh_banks.tile([P, C], F32, name="dh")
+                nc.tensor.matmul_mx(
+                    out=dh[:],
+                    lhsT=w2_code[:, e, 256 * t : 256 * (t + 1)].bitcast(E2M1X4),
+                    lhsT_scale=w2_scale[:, e, P * t : P * (t + 1)],
+                    rhs=g_code[:].bitcast(E5M2X4),
+                    rhs_scale=g_scale[:],
+                    start=True,
+                    stop=True,
+                )
+                nc.vector.tensor_tensor(y1[:, t, :], a3_t[e][:, t, :], dh[:], ALU.mult)
+                nc.vector.scalar_tensor_tensor(y3[:, t, :], a1_t[e][:, t, :], 0.0, dh[:], ALU.max, ALU.mult)
+            y1_mix = ring.tile([P, C, PACK], BF16, name="y1_mix", align_bytes=64)
+            interleave(y1_mix[:], y1[:])
+            y3_mix = ring.tile([P, C, PACK], BF16, name="y3_mix", align_bytes=64)
+            interleave(y3_mix[:], y3[:])
+            code1, scale1 = quantise(y1_mix[:], "d1")
+            code3, scale3 = quantise(y3_mix[:], "d3")
+
+            for k in range(K // P):
+                acc = dx_banks.tile([P, C], F32, name="acc")
+                for w_code, w_scale, code, scale, first in (
+                    (w1_code, w1_scale, code1, scale1, True),
+                    (w3_code, w3_scale, code3, scale3, False),
+                ):
+                    nc.tensor.matmul_mx(
+                        out=acc[:],
+                        lhsT=w_code[:, e, 256 * k : 256 * (k + 1)].bitcast(E2M1X4),
+                        lhsT_scale=w_scale[:, e, P * k : P * (k + 1)],
+                        rhs=code[:].bitcast(E5M2X4),
+                        rhs_scale=scale[:],
+                        start=first,
+                        stop=not first,
+                    )
+                dx_e = dx_ring.tile([P, C], F32, name="dx_e")
+                nc.scalar.copy(dx_e[:], acc[:])
+                dx[e, k] = dx_e
+
+        windows = [held.tile([P, T], F32, name=f"window_{k}") for k in range(K // P)]
+
+        def scatter(e, k):
+            idx = offsets[:, e * (C // 16) : (e + 1) * (C // 16)]
+            nc.vector.tensor_copy(windows[k][:].indirect(idx), dx[e, k][:])
+
+        for e in range(E):
+            chain(e)
+            if e > 0:
+                for k in range(K // P):
+                    scatter(e - 1, k)
+        for k in range(K // P):
+            scatter(E - 1, k)
+            nc.sync.dma_start(out[k * P : (k + 1) * P, :], windows[k][:])

@@ -3,11 +3,16 @@ from contextlib import ExitStack
 import concourse.mybir as mybir
 
 K, T, E, C, H, N = 256, 2048, 4, 512, 512, 512
+
 P = 128
 PACK = 4
+K_BLOCKS = K // P
+LIST_ROWS = 16
+RUN = 4
 
 FLOPS = 2 * E * C * (N * H + 2 * H * K)
-BYTES = 4 * (N * T + 2 * H * E * C + E * C + K * T) + E * (N * H + 2 * H * K) // 2 + E * (N * H + 2 * H * K) // 32 + 2 * P * T // 16
+WEIGHTS = E * (N * H + 2 * H * K)
+BYTES = 4 * (N * T + 2 * H * E * C + E * C + K * T) + WEIGHTS // 2 + WEIGHTS // 32 + 2 * P * (E * C // LIST_ROWS)
 
 F32 = mybir.dt.float32
 BF16 = mybir.dt.bfloat16
@@ -17,8 +22,10 @@ U16 = mybir.dt.uint16
 U8 = mybir.dt.uint8
 E5M2X4 = mybir.dt.float8_e5m2_x4
 E2M1X4 = mybir.dt.float4_e2m1fn_x4
-ALU = mybir.AluOpType
+MULT = mybir.AluOpType.mult
 COPY = mybir.ActivationFunctionType.Copy
+RELU = mybir.ActivationFunctionType.Relu
+SIGN = mybir.ActivationFunctionType.Sign
 
 
 def tile_moe_bdx_glu_relu_kernel(
@@ -27,145 +34,197 @@ def tile_moe_bdx_glu_relu_kernel(
     nc = tc.nc
     with ExitStack() as ctx:
         held = ctx.enter_context(tc.tile_pool(name="held", bufs=1))
+        token_wide = ctx.enter_context(tc.tile_pool(name="token_wide", bufs=PACK))
+        gathered = ctx.enter_context(tc.tile_pool(name="gathered", bufs=E))
         ring = ctx.enter_context(tc.tile_pool(name="ring", bufs=2))
-        dx_ring = ctx.enter_context(tc.tile_pool(name="dx_ring", bufs=6))
+        saved = ctx.enter_context(tc.tile_pool(name="saved", bufs=3))
         dh_banks = ctx.enter_context(tc.psum_pool(name="dh_banks", bufs=6))
         dx_banks = ctx.enter_context(tc.psum_pool(name="dx_banks", bufs=2))
-
-        offsets = held.tile([P, E * C // 16], U16, name="offsets")
-        nc.sync.dma_start(offsets[:], offs)
-
-        def load_scales(plane, dram):
-            for q in range(4):
-                nc.sync.dma_start(
-                    plane[32 * q : 32 * q + 4].bitcast(I32),
-                    dram[:, 0, 4 * q : 4 * q + 4, :].rearrange("e f i -> f e i").bitcast(I32),
-                )
-
-        w2_raw = held.tile([P, E, 2 * H], U8, name="w2_raw", align_bytes=64)
-        w2_raw_scale = held.tile([P, E, H], U8, name="w2_raw_scale", align_bytes=64)
-        w2_code = held.tile([P, E, 2 * H], U8, name="w2_code", align_bytes=64)
-        w2_scale = held.tile([P, E, H], U8, name="w2_scale", align_bytes=64)
-        w1_code = held.tile([P, E, 2 * K], U8, name="w1_code", align_bytes=64)
-        w3_code = held.tile([P, E, 2 * K], U8, name="w3_code", align_bytes=64)
-        w1_scale = held.tile([P, E, K], U8, name="w1_scale", align_bytes=64)
-        w3_scale = held.tile([P, E, K], U8, name="w3_scale", align_bytes=64)
-        for plane in (w2_raw_scale, w1_scale, w3_scale):
-            nc.vector.memset(plane[:].bitcast(I32), 0)
-
-        gates = held.tile([P, E * C], F32, name="gates")
-        planes = [held.tile([P, T], F32, name=f"dy_{j}") for j in range(PACK)]
-        a1_t = [held.tile([P, PACK, C], F32, name=f"a1_{e}") for e in range(E)]
-        a3_t = [held.tile([P, PACK, C], F32, name=f"a3_{e}") for e in range(E)]
 
         def slots(e):
             return slice(e * C, (e + 1) * C)
 
-        def load_saved(e):
-            nc.sync.dma_start(a1_t[e][:], a1.rearrange("(p t) s -> p t s", t=PACK)[:, :, slots(e)])
-            nc.sync.dma_start(a3_t[e][:], a3.rearrange("(p t) s -> p t s", t=PACK)[:, :, slots(e)])
+        offsets = held.tile([P, E * C // LIST_ROWS], U16, name="offsets")
+        nc.sync.dma_start(offsets[:], offs)
 
-        nc.sync.dma_start(w2_raw[:].bitcast(I32), w2_words.rearrange("e s p b -> p (e s) b").bitcast(I32))
-        load_scales(w2_raw_scale, w2_scales)
-        nc.sync.dma_start(gates[:, 0 : 2 * C], gate[0:P, 0 : 2 * C])
-        for j in range(PACK):
-            nc.sync.dma_start(planes[j][:], dyT.rearrange("(p j) s -> p j s", j=PACK)[:, j, :])
-        load_saved(0)
-        nc.sync.dma_start(gates[:, 2 * C : 4 * C], gate[0:P, 2 * C : 4 * C])
-        nc.sync.dma_start(w1_code[:].bitcast(I32), w1_words.rearrange("e s p b -> p (e s) b").bitcast(I32))
-        nc.sync.dma_start(w3_code[:].bitcast(I32), w3_words.rearrange("e s p b -> p (e s) b").bitcast(I32))
+        def entries(e):
+            return offsets[:, e * C // LIST_ROWS : (e + 1) * C // LIST_ROWS]
+
+        def load_words(tile, dram):
+            nc.sync.dma_start(tile[:].bitcast(I32), dram.rearrange("e s p b -> p (e s) b").bitcast(I32))
+
+        def load_scales(tile, dram):
+            for q in range(4):
+                nc.sync.dma_start(
+                    tile[32 * q : 32 * q + 4].bitcast(I32),
+                    dram[:, 0, 4 * q : 4 * q + 4, :].rearrange("e f i -> f e i").bitcast(I32),
+                )
+
+        w2_arrived = held.tile([P, E, 2 * H], U8, name="w2_arrived", align_bytes=64)
+        w2_arrived_scale = held.tile([P, E, H], U8, name="w2_arrived_scale", align_bytes=64)
+        w2_code = held.tile([P, E, 2 * H], U8, name="w2_code", align_bytes=64)
+        w2_scale = held.tile([P, E, H], U8, name="w2_scale", align_bytes=64)
+        w1_code = held.tile([P, E, 2 * K], U8, name="w1_code", align_bytes=64)
+        w1_scale = held.tile([P, E, K], U8, name="w1_scale", align_bytes=64)
+        w3_code = held.tile([P, E, 2 * K], U8, name="w3_code", align_bytes=64)
+        w3_scale = held.tile([P, E, K], U8, name="w3_scale", align_bytes=64)
+        for tile in (w2_arrived_scale, w1_scale, w3_scale):
+            nc.gpsimd.memset(tile[:].bitcast(I32), 0)
+
+        gates = held.tile([P, E * C], F32, name="gates")
+        dy_planes = {}
+        a1_saved, a3_saved = {}, {}
+
+        def load_gates(first, last):
+            columns = slice(first * C, (last + 1) * C)
+            nc.sync.dma_start(gates[:, columns], gate[0:P, columns])
+
+        def load_plane(j):
+            dy_planes[j] = token_wide.tile([P, T], F32, name="token_wide_tile")
+            nc.sync.dma_start(dy_planes[j][:], dyT.rearrange("(p j) s -> p j s", j=PACK)[:, j, :])
+
+        def load_saved(tiles, dram, e, name):
+            tiles[e] = saved.tile([P, PACK, C], F32, name=name)
+            nc.sync.dma_start(tiles[e][:], dram.rearrange("(p t) s -> p t s", t=PACK)[:, :, slots(e)])
+
+        def load_a1(e):
+            load_saved(a1_saved, a1, e, "a1_saved")
+
+        def load_a3(e):
+            load_saved(a3_saved, a3, e, "a3_saved")
+
+        load_words(w2_arrived, w2_words)
+        load_scales(w2_arrived_scale, w2_scales)
+        load_gates(0, 0)
+        load_plane(0)
+        load_gates(1, 1)
+        for j in range(1, PACK):
+            load_plane(j)
+        load_a1(0)
+        load_a3(0)
+        load_gates(2, 3)
+        load_a1(1)
+        load_a3(1)
+        load_words(w1_code, w1_words)
+        load_words(w3_code, w3_words)
         load_scales(w1_scale, w1_scales)
         load_scales(w3_scale, w3_scales)
-        for e in range(1, E):
-            load_saved(e)
+        load_a1(2)
+        load_a3(2)
 
         nc.vector.tensor_copy(
             w2_code[:].bitcast(U16).rearrange("p e (t m) -> p e t m", t=PACK),
-            w2_raw[:].bitcast(U16).rearrange("p e (m t) -> p e t m", t=PACK),
+            w2_arrived[:].bitcast(U16).rearrange("p e (m t) -> p e t m", t=PACK),
         )
         nc.vector.tensor_copy(
             w2_scale[:].rearrange("p e (t m) -> p e t m", t=PACK),
-            w2_raw_scale[:].rearrange("p e (m t) -> p e t m", t=PACK),
+            w2_arrived_scale[:].rearrange("p e (m t) -> p e t m", t=PACK),
         )
 
-        def interleave(dst, src):
-            nc.scalar.activation(
-                dst.rearrange("p (c i) t -> p c t i", i=4), src.rearrange("p t (c i) -> p c t i", i=4), COPY
-            )
+        def from_rows(ap):
+            return ap.rearrange("p t (c i) -> p c t i", i=RUN)
 
-        def quantise(values, kind):
-            code = ring.tile([P, C], U32, name=f"{kind}_code", align_bytes=64)
-            scale = ring.tile([P, C], U8, name=f"{kind}_scale", align_bytes=64)
+        def to_columns(ap):
+            return ap.rearrange("p (c i) t -> p c t i", i=RUN)
+
+        def quantise(values, name):
+            code = ring.tile([P, C], U32, name=name + "_code", align_bytes=64)
+            scale = ring.tile([P, C], U8, name=name + "_scale", align_bytes=64)
             nc.vector.quantize_mx(
                 out=code[:].bitcast(E5M2X4), scales=scale[:], in_=values.rearrange("p c t -> p (c t)")
             )
             return code, scale
 
-        dx = {}
+        gradients, gradient_codes, zero_one, da1_rounded, da3_rounded, dx = {}, {}, {}, {}, {}, {}
 
-        def chain(e):
-            idx = offsets[:, e * (C // 16) : (e + 1) * (C // 16)]
-            g4 = ring.tile([P, PACK, C], F32, name="g4")
+        def gather(e):
+            gradients[e] = gathered.tile([P, PACK, C], F32, name="gradients_tile")
             for j in range(PACK):
-                nc.vector.tensor_tensor(g4[:, j, :], planes[j][:].indirect(idx), gates[:, slots(e)], ALU.mult)
-            g_mix = ring.tile([P, C, PACK], BF16, name="g_mix", align_bytes=64)
-            interleave(g_mix[:], g4[:])
-            g_code, g_scale = quantise(g_mix[:], "g")
+                nc.vector.tensor_tensor(
+                    gradients[e][:, j, :], dy_planes[j][:].indirect(entries(e)), gates[:, slots(e)], MULT
+                )
 
-            nc.vector.scalar_tensor_tensor(a3_t[e][:], a1_t[e][:], 0.0, a3_t[e][:], ALU.is_gt, ALU.mult)
+        def apply_relu(e):
+            nc.scalar.activation(a1_saved[e][:], a1_saved[e][:], RELU)
+            zero_one[e] = ring.tile([P, C, PACK], BF16, name="zero_one_tile")
+            nc.scalar.activation(to_columns(zero_one[e][:]), from_rows(a1_saved[e][:]), SIGN)
 
-            y1 = ring.tile([P, PACK, C], BF16, name="y1")
-            y3 = ring.tile([P, PACK, C], BF16, name="y3")
+        def quantise_gradients(e):
+            rounded = ring.tile([P, C, PACK], BF16, name="g_rounded", align_bytes=64)
+            nc.scalar.activation(to_columns(rounded[:]), from_rows(gradients[e][:]), COPY)
+            gradient_codes[e] = quantise(rounded[:], "g")
+
+        def hidden_gradients(e):
+            code, scale = gradient_codes[e]
+            dh = ring.tile([P, PACK, C], F32, name="dh")
             for t in range(PACK):
-                dh = dh_banks.tile([P, C], F32, name="dh")
+                bank = dh_banks.tile([P, C], F32, name="dh_bank")
                 nc.tensor.matmul_mx(
-                    out=dh[:],
-                    lhsT=w2_code[:, e, 256 * t : 256 * (t + 1)].bitcast(E2M1X4),
+                    out=bank[:],
+                    lhsT=w2_code[:, e, 2 * P * t : 2 * P * (t + 1)].bitcast(E2M1X4),
                     lhsT_scale=w2_scale[:, e, P * t : P * (t + 1)],
-                    rhs=g_code[:].bitcast(E5M2X4),
-                    rhs_scale=g_scale[:],
+                    rhs=code[:].bitcast(E5M2X4),
+                    rhs_scale=scale[:],
                     start=True,
                     stop=True,
                 )
-                nc.vector.tensor_tensor(y1[:, t, :], a3_t[e][:, t, :], dh[:], ALU.mult)
-                nc.vector.scalar_tensor_tensor(y3[:, t, :], a1_t[e][:, t, :], 0.0, dh[:], ALU.max, ALU.mult)
-            y1_mix = ring.tile([P, C, PACK], BF16, name="y1_mix", align_bytes=64)
-            interleave(y1_mix[:], y1[:])
-            y3_mix = ring.tile([P, C, PACK], BF16, name="y3_mix", align_bytes=64)
-            interleave(y3_mix[:], y3[:])
-            code1, scale1 = quantise(y1_mix[:], "d1")
-            code3, scale3 = quantise(y3_mix[:], "d3")
+                nc.scalar.copy(dh[:, t, :], bank[:])
+            da1_rounded[e] = ring.tile([P, C, PACK], BF16, name="da1_rounded", align_bytes=64)
+            da3_rounded[e] = ring.tile([P, C, PACK], BF16, name="da3_rounded", align_bytes=64)
+            for rounded, factor in ((da1_rounded[e], a3_saved[e]), (da3_rounded[e], a1_saved[e])):
+                nc.vector.tensor_tensor(to_columns(rounded[:]), from_rows(factor[:]), from_rows(dh[:]), MULT)
 
-            for k in range(K // P):
-                acc = dx_banks.tile([P, C], F32, name="acc")
+        def output_gradients(e):
+            nc.vector.tensor_tensor(da1_rounded[e][:], da1_rounded[e][:], zero_one[e][:], MULT)
+            da3_code, da3_scale = quantise(da3_rounded[e][:], "da3")
+            da1_code, da1_scale = quantise(da1_rounded[e][:], "da1")
+            for k in range(K_BLOCKS):
+                bank = dx_banks.tile([P, C], F32, name="dx_bank")
                 for w_code, w_scale, code, scale, first in (
-                    (w1_code, w1_scale, code1, scale1, True),
-                    (w3_code, w3_scale, code3, scale3, False),
+                    (w3_code, w3_scale, da3_code, da3_scale, True),
+                    (w1_code, w1_scale, da1_code, da1_scale, False),
                 ):
                     nc.tensor.matmul_mx(
-                        out=acc[:],
-                        lhsT=w_code[:, e, 256 * k : 256 * (k + 1)].bitcast(E2M1X4),
+                        out=bank[:],
+                        lhsT=w_code[:, e, 2 * P * k : 2 * P * (k + 1)].bitcast(E2M1X4),
                         lhsT_scale=w_scale[:, e, P * k : P * (k + 1)],
                         rhs=code[:].bitcast(E5M2X4),
                         rhs_scale=scale[:],
                         start=first,
                         stop=not first,
                     )
-                dx_e = dx_ring.tile([P, C], F32, name="dx_e")
-                nc.scalar.copy(dx_e[:], acc[:])
-                dx[e, k] = dx_e
+                dx[e, k] = held.tile([P, C], F32, name=f"dx_{e}_{k}")
+                nc.scalar.copy(dx[e, k][:], bank[:])
 
-        windows = [held.tile([P, T], F32, name=f"window_{k}") for k in range(K // P)]
+        windows = {}
 
         def scatter(e, k):
-            idx = offsets[:, e * (C // 16) : (e + 1) * (C // 16)]
-            nc.vector.tensor_copy(windows[k][:].indirect(idx), dx[e, k][:])
+            if k not in windows:
+                windows[k] = token_wide.tile([P, T], F32, name="token_wide_tile")
+            nc.vector.tensor_copy(windows[k][:].indirect(entries(e)), dx[e, k][:])
 
-        for e in range(E):
-            chain(e)
-            if e > 0:
-                for k in range(K // P):
-                    scatter(e - 1, k)
-        for k in range(K // P):
-            scatter(E - 1, k)
+        def expert(e):
+            apply_relu(e)
+            quantise_gradients(e)
+            hidden_gradients(e)
+            output_gradients(e)
+
+        gather(0)
+        gather(1)
+        expert(0)
+        load_a1(3)
+        load_a3(3)
+        expert(1)
+        scatter(0, 0)
+        scatter(0, 1)
+        gather(2)
+        gather(3)
+        expert(2)
+        scatter(1, 0)
+        scatter(1, 1)
+        expert(3)
+        scatter(2, 0)
+        scatter(2, 1)
+        for k in range(K_BLOCKS):
+            scatter(3, k)
             nc.sync.dma_start(out[k * P : (k + 1) * P, :], windows[k][:])

from contextlib import ExitStack

import concourse.mybir as mybir

K, T, E, C, H, N = 256, 2048, 4, 512, 512, 512

P = 128
PACK = 4
K_BLOCKS = K // P
LIST_ROWS = 16
RUN = 4

FLOPS = 2 * E * C * (N * H + 2 * H * K)
WEIGHTS = E * (N * H + 2 * H * K)
BYTES = 4 * (N * T + 2 * H * E * C + E * C + K * T) + WEIGHTS // 2 + WEIGHTS // 32 + 2 * P * (E * C // LIST_ROWS)

F32 = mybir.dt.float32
BF16 = mybir.dt.bfloat16
I32 = mybir.dt.int32
U32 = mybir.dt.uint32
U16 = mybir.dt.uint16
U8 = mybir.dt.uint8
E5M2X4 = mybir.dt.float8_e5m2_x4
E2M1X4 = mybir.dt.float4_e2m1fn_x4
MULT = mybir.AluOpType.mult
COPY = mybir.ActivationFunctionType.Copy
RELU = mybir.ActivationFunctionType.Relu
SIGN = mybir.ActivationFunctionType.Sign


def tile_moe_bdx_glu_relu_kernel(
    tc, dyT, a1, a3, w2_words, w2_scales, w1_words, w1_scales, w3_words, w3_scales, gate, offs, out
):
    nc = tc.nc
    with ExitStack() as ctx:
        held = ctx.enter_context(tc.tile_pool(name="held", bufs=1))
        token_wide = ctx.enter_context(tc.tile_pool(name="token_wide", bufs=PACK))
        gathered = ctx.enter_context(tc.tile_pool(name="gathered", bufs=E))
        ring = ctx.enter_context(tc.tile_pool(name="ring", bufs=2))
        saved = ctx.enter_context(tc.tile_pool(name="saved", bufs=3))
        dh_banks = ctx.enter_context(tc.psum_pool(name="dh_banks", bufs=6))
        dx_banks = ctx.enter_context(tc.psum_pool(name="dx_banks", bufs=2))

        def slots(e):
            return slice(e * C, (e + 1) * C)

        offsets = held.tile([P, E * C // LIST_ROWS], U16, name="offsets")
        nc.sync.dma_start(offsets[:], offs)

        def entries(e):
            return offsets[:, e * C // LIST_ROWS : (e + 1) * C // LIST_ROWS]

        def load_words(tile, dram):
            nc.sync.dma_start(tile[:].bitcast(I32), dram.rearrange("e s p b -> p (e s) b").bitcast(I32))

        def load_scales(tile, dram):
            for q in range(4):
                nc.sync.dma_start(
                    tile[32 * q : 32 * q + 4].bitcast(I32),
                    dram[:, 0, 4 * q : 4 * q + 4, :].rearrange("e f i -> f e i").bitcast(I32),
                )

        w2_arrived = held.tile([P, E, 2 * H], U8, name="w2_arrived", align_bytes=64)
        w2_arrived_scale = held.tile([P, E, H], U8, name="w2_arrived_scale", align_bytes=64)
        w2_code = held.tile([P, E, 2 * H], U8, name="w2_code", align_bytes=64)
        w2_scale = held.tile([P, E, H], U8, name="w2_scale", align_bytes=64)
        w1_code = held.tile([P, E, 2 * K], U8, name="w1_code", align_bytes=64)
        w1_scale = held.tile([P, E, K], U8, name="w1_scale", align_bytes=64)
        w3_code = held.tile([P, E, 2 * K], U8, name="w3_code", align_bytes=64)
        w3_scale = held.tile([P, E, K], U8, name="w3_scale", align_bytes=64)
        for tile in (w2_arrived_scale, w1_scale, w3_scale):
            nc.gpsimd.memset(tile[:].bitcast(I32), 0)

        gates = held.tile([P, E * C], F32, name="gates")
        dy_planes = {}
        a1_saved, a3_saved = {}, {}

        def load_gates(first, last):
            columns = slice(first * C, (last + 1) * C)
            nc.sync.dma_start(gates[:, columns], gate[0:P, columns])

        def load_plane(j):
            dy_planes[j] = token_wide.tile([P, T], F32, name="token_wide_tile")
            nc.sync.dma_start(dy_planes[j][:], dyT.rearrange("(p j) s -> p j s", j=PACK)[:, j, :])

        def load_saved(tiles, dram, e, name):
            tiles[e] = saved.tile([P, PACK, C], F32, name=name)
            nc.sync.dma_start(tiles[e][:], dram.rearrange("(p t) s -> p t s", t=PACK)[:, :, slots(e)])

        def load_a1(e):
            load_saved(a1_saved, a1, e, "a1_saved")

        def load_a3(e):
            load_saved(a3_saved, a3, e, "a3_saved")

        load_words(w2_arrived, w2_words)
        load_scales(w2_arrived_scale, w2_scales)
        load_gates(0, 0)
        load_plane(0)
        load_gates(1, 1)
        for j in range(1, PACK):
            load_plane(j)
        load_a1(0)
        load_a3(0)
        load_gates(2, 3)
        load_a1(1)
        load_a3(1)
        load_words(w1_code, w1_words)
        load_words(w3_code, w3_words)
        load_scales(w1_scale, w1_scales)
        load_scales(w3_scale, w3_scales)
        load_a1(2)
        load_a3(2)

        nc.vector.tensor_copy(
            w2_code[:].bitcast(U16).rearrange("p e (t m) -> p e t m", t=PACK),
            w2_arrived[:].bitcast(U16).rearrange("p e (m t) -> p e t m", t=PACK),
        )
        nc.vector.tensor_copy(
            w2_scale[:].rearrange("p e (t m) -> p e t m", t=PACK),
            w2_arrived_scale[:].rearrange("p e (m t) -> p e t m", t=PACK),
        )

        def from_rows(ap):
            return ap.rearrange("p t (c i) -> p c t i", i=RUN)

        def to_columns(ap):
            return ap.rearrange("p (c i) t -> p c t i", i=RUN)

        def quantise(values, name):
            code = ring.tile([P, C], U32, name=name + "_code", align_bytes=64)
            scale = ring.tile([P, C], U8, name=name + "_scale", align_bytes=64)
            nc.vector.quantize_mx(
                out=code[:].bitcast(E5M2X4), scales=scale[:], in_=values.rearrange("p c t -> p (c t)")
            )
            return code, scale

        gradients, gradient_codes, zero_one, da1_rounded, da3_rounded, dx = {}, {}, {}, {}, {}, {}

        def gather(e):
            gradients[e] = gathered.tile([P, PACK, C], F32, name="gradients_tile")
            for j in range(PACK):
                nc.vector.tensor_tensor(
                    gradients[e][:, j, :], dy_planes[j][:].indirect(entries(e)), gates[:, slots(e)], MULT
                )

        def apply_relu(e):
            nc.scalar.activation(a1_saved[e][:], a1_saved[e][:], RELU)
            zero_one[e] = ring.tile([P, C, PACK], BF16, name="zero_one_tile")
            nc.scalar.activation(to_columns(zero_one[e][:]), from_rows(a1_saved[e][:]), SIGN)

        def quantise_gradients(e):
            rounded = ring.tile([P, C, PACK], BF16, name="g_rounded", align_bytes=64)
            nc.scalar.activation(to_columns(rounded[:]), from_rows(gradients[e][:]), COPY)
            gradient_codes[e] = quantise(rounded[:], "g")

        def hidden_gradients(e):
            code, scale = gradient_codes[e]
            dh = ring.tile([P, PACK, C], F32, name="dh")
            for t in range(PACK):
                bank = dh_banks.tile([P, C], F32, name="dh_bank")
                nc.tensor.matmul_mx(
                    out=bank[:],
                    lhsT=w2_code[:, e, 2 * P * t : 2 * P * (t + 1)].bitcast(E2M1X4),
                    lhsT_scale=w2_scale[:, e, P * t : P * (t + 1)],
                    rhs=code[:].bitcast(E5M2X4),
                    rhs_scale=scale[:],
                    start=True,
                    stop=True,
                )
                nc.scalar.copy(dh[:, t, :], bank[:])
            da1_rounded[e] = ring.tile([P, C, PACK], BF16, name="da1_rounded", align_bytes=64)
            da3_rounded[e] = ring.tile([P, C, PACK], BF16, name="da3_rounded", align_bytes=64)
            for rounded, factor in ((da1_rounded[e], a3_saved[e]), (da3_rounded[e], a1_saved[e])):
                nc.vector.tensor_tensor(to_columns(rounded[:]), from_rows(factor[:]), from_rows(dh[:]), MULT)

        def output_gradients(e):
            nc.vector.tensor_tensor(da1_rounded[e][:], da1_rounded[e][:], zero_one[e][:], MULT)
            da3_code, da3_scale = quantise(da3_rounded[e][:], "da3")
            da1_code, da1_scale = quantise(da1_rounded[e][:], "da1")
            for k in range(K_BLOCKS):
                bank = dx_banks.tile([P, C], F32, name="dx_bank")
                for w_code, w_scale, code, scale, first in (
                    (w3_code, w3_scale, da3_code, da3_scale, True),
                    (w1_code, w1_scale, da1_code, da1_scale, False),
                ):
                    nc.tensor.matmul_mx(
                        out=bank[:],
                        lhsT=w_code[:, e, 2 * P * k : 2 * P * (k + 1)].bitcast(E2M1X4),
                        lhsT_scale=w_scale[:, e, P * k : P * (k + 1)],
                        rhs=code[:].bitcast(E5M2X4),
                        rhs_scale=scale[:],
                        start=first,
                        stop=not first,
                    )
                dx[e, k] = held.tile([P, C], F32, name=f"dx_{e}_{k}")
                nc.scalar.copy(dx[e, k][:], bank[:])

        windows = {}

        def scatter(e, k):
            if k not in windows:
                windows[k] = token_wide.tile([P, T], F32, name="token_wide_tile")
            nc.vector.tensor_copy(windows[k][:].indirect(entries(e)), dx[e, k][:])

        def expert(e):
            apply_relu(e)
            quantise_gradients(e)
            hidden_gradients(e)
            output_gradients(e)

        gather(0)
        gather(1)
        expert(0)
        load_a1(3)
        load_a3(3)
        expert(1)
        scatter(0, 0)
        scatter(0, 1)
        gather(2)
        gather(3)
        expert(2)
        scatter(1, 0)
        scatter(1, 1)
        expert(3)
        scatter(2, 0)
        scatter(2, 1)
        for k in range(K_BLOCKS):
            scatter(3, k)
            nc.sync.dma_start(out[k * P : (k + 1) * P, :], windows[k][:])
